import numpy as np
import ml_dtypes


def mxq(x, axis, fmt="e4m3"):
    dtype, down = {"e4m3": (ml_dtypes.float8_e4m3fn, 7), "e5m2": (ml_dtypes.float8_e5m2, 14)}[fmt]
    v = np.moveaxis(np.asarray(x, np.float32).astype(ml_dtypes.bfloat16).astype(np.float64), axis, -1)
    blocks = v.reshape(v.shape[:-1] + (-1, 32))
    amax = np.abs(blocks).max(-1, keepdims=True)
    byte = np.maximum(np.where(amax > 0, np.frexp(amax)[1] - 1 + 127, 0) - down, 1)
    scale = np.exp2(byte - 127.0)
    codes = (blocks / scale).astype(np.float32).astype(dtype).astype(np.float64)
    return np.moveaxis((codes * scale).reshape(v.shape), -1, axis)


WIDE = False


def mx_kscale(k, group=512):
    if not WIDE:
        return np.ones(k)
    levels = np.array([10, -10, 5, -5, 0])
    if group != 512:
        return np.exp2(np.random.permutation(np.resize(levels, k // group))).repeat(group)
    if k % 512:
        return np.exp2(np.random.permutation(np.resize(levels, k // 32))).repeat(32)
    a = np.empty((k // 512, 16))
    for p in range(k // 512):
        a[p, :8] = np.random.permutation(np.resize(levels, 8))
        for g in range(8):
            far = levels[np.abs(levels - a[p, g]) >= 10]
            a[p, g + 8] = far[np.random.randint(len(far))]
    return np.exp2(a.ravel()).repeat(32)


def f64(x):
    return np.asarray(x).astype(np.float64)


G, D, M, N = 2, 256, 256, 512


def setup_inputs():
    n = np.random.standard_normal
    s = mx_kscale(D, 0)[:, None]
    return {
        "x": (n((G, D, N)) * s).astype(np.float32),
        "w": (n((G, D, M)) / np.sqrt(D) / s).astype(np.float32),
        "u": (n((G, D, M)) / np.sqrt(D) / s).astype(np.float32),
        "b": (0.5 * n((G, M, 1))).astype(np.float32),
        "r": n((G, M, N)).astype(np.float32),
    }


def reference(x, w, u, b, r):
    xq = mxq(f64(x), 1, "e4m3")
    h = mxq(f64(w), 1, "e4m3").transpose(0, 2, 1) @ xq
    g = mxq(f64(u), 1, "e4m3").transpose(0, 2, 1) @ xq
    h = h + f64(b)
    y = 1.0 / (1.0 + np.exp(-(h))) * g
    y = y + f64(r)
    return y

@@ -1,0 +1,147 @@
+from contextlib import ExitStack
+
+import concourse.mybir as mybir
+
+G, D, M, N = 2, 256, 256, 512
+FLOPS = 2 * 2 * G * D * M * N
+
+F32 = mybir.dt.float32
+BF16 = mybir.dt.bfloat16
+U32 = mybir.dt.uint32
+U8 = mybir.dt.uint8
+FP8X4 = mybir.dt.float8_e4m3fn_x4
+ACT = mybir.ActivationFunctionType
+ALU = mybir.AluOpType
+
+P = 128
+PACK = 4
+ROWS = D // PACK
+MT = 128
+TILES = M // MT
+HALF = N // 2
+X_VECTOR = 96
+
+
+def walk(raw, grouped):
+    src = raw.rearrange("p j (c i) -> p c j i", i=4)
+    dst = grouped.rearrange("p (c i) j -> p c j i", i=4)
+    return dst, src
+
+
+def interleave_vector(nc, raw, grouped):
+    dst, src = walk(raw, grouped)
+    nc.vector.tensor_copy(out=dst, in_=src)
+
+
+def interleave_scalar(nc, raw, grouped):
+    dst, src = walk(raw, grouped)
+    nc.scalar.copy(out=dst, in_=src)
+
+
+def quantize(nc, grouped, codes, scales):
+    nc.vector.quantize_mx(
+        out=codes.bitcast(FP8X4),
+        scales=scales,
+        in_=grouped.rearrange("p c j -> p (c j)"),
+    )
+
+
+def tile_rows_gglu_sigmoid_bias_res_kernel(tc, x, w, u, b, r, out):
+    nc = tc.nc
+    with ExitStack() as ctx:
+        sb = ctx.enter_context(tc.tile_pool(name="sb", bufs=1))
+        ps = ctx.enter_context(tc.psum_pool(name="ps", bufs=1))
+        ctx.enter_context(tc.manual_schedule())
+
+        order = [(g, t) for t in range(TILES) for g in range(G)]
+
+        x_raw = sb.tile([P, PACK, N], F32, name="x_raw")
+        w_raw = sb.tile([P, PACK, M], F32, name="w_raw")
+        u_raw = sb.tile([P, PACK, M], F32, name="u_raw")
+        nc.sync.dma_start(out=x_raw[:], in_=x.rearrange("g (p j) n -> (g p) j n", j=PACK))
+        nc.sync.dma_start(out=w_raw[:], in_=w.rearrange("g (p j) m -> (g p) j m", j=PACK))
+        nc.sync.dma_start(out=u_raw[:], in_=u.rearrange("g (p j) m -> (g p) j m", j=PACK))
+        res = {}
+        for g, t in order:
+            res[g, t] = sb.tile([P, N], F32, name="res_%d_%d" % (g, t))
+            nc.sync.dma_start(out=res[g, t][:], in_=r[g, t * MT:(t + 1) * MT, :])
+
+        b_rows = sb.tile([P, P], F32, name="b_rows", align_bytes=64)
+        b_cols = sb.tile([P, P], F32, name="b_cols", align_bytes=64)
+        bias = sb.tile([P, G * TILES], F32, name="bias")
+        nc.vector.memset(b_rows[:], 0.0)
+        nc.scalar.dma_start(
+            out=b_rows[0:P:32, :].rearrange("q (a i) -> q a i", i=32),
+            in_=b.rearrange("g (t q i) o -> q (g t) (i o)", t=TILES, i=32),
+        )
+        nc.vector.transpose(out=b_cols[:], in_=b_rows[:])
+        nc.vector.tensor_scalar(out=bias[:], in0=b_cols[:, 0:P:32], scalar1=0.5, scalar2=None, op0=ALU.mult)
+
+        x_lo = sb.tile([P, HALF, PACK], BF16, name="x_lo", align_bytes=64)
+        x_hi = sb.tile([P, HALF, PACK], BF16, name="x_hi", align_bytes=64)
+        x_codes = sb.tile([P, N], U32, name="x_codes", align_bytes=64)
+        x_scales = sb.tile([P, N], U8, name="x_scales", align_bytes=64)
+        interleave_vector(nc, x_raw[:, :, 0:HALF], x_lo[:])
+        interleave_scalar(nc, x_raw[:, :, HALF + X_VECTOR:N], x_hi[:, X_VECTOR:HALF, :])
+        interleave_vector(nc, x_raw[:, :, HALF:HALF + X_VECTOR], x_hi[:, 0:X_VECTOR, :])
+        quantize(nc, x_lo[:], x_codes[:, 0:HALF], x_scales[:, 0:HALF])
+        quantize(nc, x_hi[:], x_codes[:, HALF:N], x_scales[:, HALF:N])
+
+        grouped, codes, scales = {}, {}, {}
+        for name in ("w", "u"):
+            for t in range(TILES):
+                grouped[name, t] = sb.tile([P, MT, PACK], BF16, name="%s_bf_%d" % (name, t), align_bytes=64)
+                codes[name, t] = sb.tile([P, MT], U32, name="%s_codes_%d" % (name, t), align_bytes=64)
+                scales[name, t] = sb.tile([P, MT], U8, name="%s_scales_%d" % (name, t), align_bytes=64)
+
+        interleave_scalar(nc, w_raw[:, :, 0:MT], grouped["w", 0][:])
+        interleave_vector(nc, w_raw[:, :, MT:M], grouped["w", 1][:])
+        for t in range(TILES):
+            quantize(nc, grouped["w", t][:], codes["w", t][:], scales["w", t][:])
+        for t in range(TILES):
+            interleave_vector(nc, u_raw[:, :, t * MT:(t + 1) * MT], grouped["u", t][:])
+        for t in range(TILES):
+            quantize(nc, grouped["u", t][:], codes["u", t][:], scales["u", t][:])
+
+        acc = {}
+        for t in range(TILES):
+            for name in ("w", "u"):
+                for g in range(G):
+                    rows = slice(g * ROWS, (g + 1) * ROWS)
+                    acc[name, g, t] = ps.tile([P, N], F32, name="acc_%s_%d_%d" % (name, g, t))
+                    nc.tensor.matmul_mx(
+                        out=acc[name, g, t][:],
+                        lhsT=codes[name, t][rows, :].bitcast(FP8X4),
+                        lhsT_scale=scales[name, t][rows, :],
+                        rhs=x_codes[rows, :].bitcast(FP8X4),
+                        rhs_scale=x_scales[rows, :],
+                        start=True,
+                        stop=True,
+                    )
+
+        gate, prod = {}, {}
+        for g, t in order:
+            col = g * TILES + t
+            gate[g, t] = sb.tile([P, N], F32, name="gate_%d_%d" % (g, t))
+            nc.scalar.activation(
+                out=gate[g, t][:], in_=acc["w", g, t][:], func=ACT.Tanh, bias=bias[:, col:col + 1], scale=0.5
+            )
+
+        def multiply(g, t):
+            prod[g, t] = sb.tile([P, N], F32, name="prod_%d_%d" % (g, t))
+            nc.vector.scalar_tensor_tensor(
+                out=prod[g, t][:], in0=gate[g, t][:], scalar=1.0, in1=acc["u", g, t][:], op0=ALU.add, op1=ALU.mult
+            )
+
+        def finish(g, t):
+            y = sb.tile([P, N], F32, name="y_%d_%d" % (g, t))
+            nc.vector.scalar_tensor_tensor(
+                out=y[:], in0=prod[g, t][:], scalar=0.5, in1=res[g, t][:], op0=ALU.mult, op1=ALU.add
+            )
+            nc.sync.dma_start(out=out[g, t * MT:(t + 1) * MT, :], in_=y[:])
+
+        multiply(*order[0])
+        for i in range(1, len(order)):
+            multiply(*order[i])
+            finish(*order[i - 1])
+        finish(*order[-1])

@@ -58,24 +58,21 @@ def tile_rows_gglu_sigmoid_bias_res_kernel(tc, x, w, u, b, r, out):
         x_raw = sb.tile([P, PACK, N], F32, name="x_raw")
         w_raw = sb.tile([P, PACK, M], F32, name="w_raw")
         u_raw = sb.tile([P, PACK, M], F32, name="u_raw")
+        b_rows = sb.tile([P, P], F32, name="b_rows", align_bytes=64)
+        b_half = sb.tile([P, P], F32, name="b_half", align_bytes=64)
+        bias = sb.tile([P, P], F32, name="bias", align_bytes=64)
+        nc.vector.memset(b_rows[:], 0.0)
         nc.sync.dma_start(out=x_raw[:], in_=x.rearrange("g (p j) n -> (g p) j n", j=PACK))
+        nc.sync.dma_start(
+            out=b_rows[0:P:32, :].rearrange("q (a i) -> q a i", i=32),
+            in_=b.rearrange("g (t q i) o -> q (g t) (i o)", t=TILES, i=32),
+        )
         nc.sync.dma_start(out=w_raw[:], in_=w.rearrange("g (p j) m -> (g p) j m", j=PACK))
         nc.sync.dma_start(out=u_raw[:], in_=u.rearrange("g (p j) m -> (g p) j m", j=PACK))
         res = {}
         for g, t in order:
             res[g, t] = sb.tile([P, N], F32, name="res_%d_%d" % (g, t))
             nc.sync.dma_start(out=res[g, t][:], in_=r[g, t * MT:(t + 1) * MT, :])
-
-        b_rows = sb.tile([P, P], F32, name="b_rows", align_bytes=64)
-        b_cols = sb.tile([P, P], F32, name="b_cols", align_bytes=64)
-        bias = sb.tile([P, G * TILES], F32, name="bias")
-        nc.vector.memset(b_rows[:], 0.0)
-        nc.scalar.dma_start(
-            out=b_rows[0:P:32, :].rearrange("q (a i) -> q a i", i=32),
-            in_=b.rearrange("g (t q i) o -> q (g t) (i o)", t=TILES, i=32),
-        )
-        nc.vector.transpose(out=b_cols[:], in_=b_rows[:])
-        nc.vector.tensor_scalar(out=bias[:], in0=b_cols[:, 0:P:32], scalar1=0.5, scalar2=None, op0=ALU.mult)
 
         x_lo = sb.tile([P, HALF, PACK], BF16, name="x_lo", align_bytes=64)
         x_hi = sb.tile([P, HALF, PACK], BF16, name="x_hi", align_bytes=64)
@@ -84,6 +81,7 @@ def tile_rows_gglu_sigmoid_bias_res_kernel(tc, x, w, u, b, r, out):
         interleave_vector(nc, x_raw[:, :, 0:HALF], x_lo[:])
         interleave_scalar(nc, x_raw[:, :, HALF + X_VECTOR:N], x_hi[:, X_VECTOR:HALF, :])
         interleave_vector(nc, x_raw[:, :, HALF:HALF + X_VECTOR], x_hi[:, 0:X_VECTOR, :])
+        nc.scalar.activation(out=b_half[:], in_=b_rows[:], func=ACT.Copy, scale=0.5)
         quantize(nc, x_lo[:], x_codes[:, 0:HALF], x_scales[:, 0:HALF])
         quantize(nc, x_hi[:], x_codes[:, HALF:N], x_scales[:, HALF:N])
 
@@ -98,50 +96,69 @@ def tile_rows_gglu_sigmoid_bias_res_kernel(tc, x, w, u, b, r, out):
         interleave_vector(nc, w_raw[:, :, MT:M], grouped["w", 1][:])
         for t in range(TILES):
             quantize(nc, grouped["w", t][:], codes["w", t][:], scales["w", t][:])
-        for t in range(TILES):
-            interleave_vector(nc, u_raw[:, :, t * MT:(t + 1) * MT], grouped["u", t][:])
+        interleave_vector(nc, u_raw[:, :, 0:MT], grouped["u", 0][:])
+        interleave_scalar(nc, u_raw[:, :, MT:M], grouped["u", 1][:])
+        nc.vector.transpose(out=bias[:], in_=b_half[:])
         for t in range(TILES):
             quantize(nc, grouped["u", t][:], codes["u", t][:], scales["u", t][:])
 
         acc = {}
-        for t in range(TILES):
-            for name in ("w", "u"):
-                for g in range(G):
-                    rows = slice(g * ROWS, (g + 1) * ROWS)
-                    acc[name, g, t] = ps.tile([P, N], F32, name="acc_%s_%d_%d" % (name, g, t))
-                    nc.tensor.matmul_mx(
-                        out=acc[name, g, t][:],
-                        lhsT=codes[name, t][rows, :].bitcast(FP8X4),
-                        lhsT_scale=scales[name, t][rows, :],
-                        rhs=x_codes[rows, :].bitcast(FP8X4),
-                        rhs_scale=x_scales[rows, :],
-                        start=True,
-                        stop=True,
-                    )
 
-        gate, prod = {}, {}
+        def product(name, g, t):
+            rows = slice(g * ROWS, (g + 1) * ROWS)
+            acc[name, g, t] = ps.tile([P, N], F32, name="acc_%s_%d_%d" % (name, g, t))
+            nc.tensor.matmul_mx(
+                out=acc[name, g, t][:],
+                lhsT=codes[name, t][rows, :].bitcast(FP8X4),
+                lhsT_scale=scales[name, t][rows, :],
+                rhs=x_codes[rows, :].bitcast(FP8X4),
+                rhs_scale=x_scales[rows, :],
+                start=True,
+                stop=True,
+            )
+
+        for name in ("w", "u"):
+            for g in range(G):
+                product(name, g, 0)
+        for g in range(G):
+            for name in ("w", "u"):
+                product(name, g, 1)
+
+        gate, prod, y = {}, {}, {}
         for g, t in order:
-            col = g * TILES + t
+            col = 32 * (g * TILES + t)
             gate[g, t] = sb.tile([P, N], F32, name="gate_%d_%d" % (g, t))
             nc.scalar.activation(
                 out=gate[g, t][:], in_=acc["w", g, t][:], func=ACT.Tanh, bias=bias[:, col:col + 1], scale=0.5
             )
-
-        def multiply(g, t):
             prod[g, t] = sb.tile([P, N], F32, name="prod_%d_%d" % (g, t))
+            y[g, t] = sb.tile([P, N], F32, name="y_%d_%d" % (g, t))
+
+        def multiply(g, t, cols):
             nc.vector.scalar_tensor_tensor(
-                out=prod[g, t][:], in0=gate[g, t][:], scalar=1.0, in1=acc["u", g, t][:], op0=ALU.add, op1=ALU.mult
+                out=prod[g, t][:, cols],
+                in0=gate[g, t][:, cols],
+                scalar=1.0,
+                in1=acc["u", g, t][:, cols],
+                op0=ALU.add,
+                op1=ALU.mult,
             )
 
-        def finish(g, t):
-            y = sb.tile([P, N], F32, name="y_%d_%d" % (g, t))
+        def finish(g, t, cols):
             nc.vector.scalar_tensor_tensor(
-                out=y[:], in0=prod[g, t][:], scalar=0.5, in1=res[g, t][:], op0=ALU.mult, op1=ALU.add
+                out=y[g, t][:, cols],
+                in0=prod[g, t][:, cols],
+                scalar=0.5,
+                in1=res[g, t][:, cols],
+                op0=ALU.mult,
+                op1=ALU.add,
             )
-            nc.sync.dma_start(out=out[g, t * MT:(t + 1) * MT, :], in_=y[:])
+            nc.sync.dma_start(out=out[g, t * MT:(t + 1) * MT, cols], in_=y[g, t][:, cols])
 
-        multiply(*order[0])
-        for i in range(1, len(order)):
-            multiply(*order[i])
-            finish(*order[i - 1])
-        finish(*order[-1])
+        pieces = [(g, t, slice(0, N)) for g, t in order[:-1]]
+        pieces.extend([(*order[-1], slice(0, HALF)), (*order[-1], slice(HALF, N))])
+        multiply(*pieces[0])
+        for i in range(1, len(pieces)):
+            multiply(*pieces[i])
+            finish(*pieces[i - 1])
+        finish(*pieces[-1])

@@ -19,7 +19,8 @@ ROWS = D // PACK
 MT = 128
 TILES = M // MT
 HALF = N // 2
-X_VECTOR = 96
+QUARTER = N // 4
+X_VECTOR = 192
 
 
 def walk(raw, grouped):
@@ -53,54 +54,72 @@ def tile_rows_gglu_sigmoid_bias_res_kernel(tc, x, w, u, b, r, out):
         ps = ctx.enter_context(tc.psum_pool(name="ps", bufs=1))
         ctx.enter_context(tc.manual_schedule())
 
-        order = [(g, t) for t in range(TILES) for g in range(G)]
-
-        x_raw = sb.tile([P, PACK, N], F32, name="x_raw")
-        w_raw = sb.tile([P, PACK, M], F32, name="w_raw")
-        u_raw = sb.tile([P, PACK, M], F32, name="u_raw")
         b_rows = sb.tile([P, P], F32, name="b_rows", align_bytes=64)
         b_half = sb.tile([P, P], F32, name="b_half", align_bytes=64)
         bias = sb.tile([P, P], F32, name="bias", align_bytes=64)
         nc.vector.memset(b_rows[:], 0.0)
-        nc.sync.dma_start(out=x_raw[:], in_=x.rearrange("g (p j) n -> (g p) j n", j=PACK))
+
+        raw, grouped = {}, {}
+
+        def load(name, src, part, width):
+            raw[name, part] = sb.tile([P, PACK, width], F32, name="%s_raw_%d" % (name, part))
+            grouped[name, part] = sb.tile([P, width, PACK], BF16, name="%s_bf_%d" % (name, part), align_bytes=64)
+            rows = src.rearrange("g (p j) c -> (g p) j c", j=PACK)
+            nc.sync.dma_start(out=raw[name, part][:], in_=rows[:, :, part * width:(part + 1) * width])
+
+        load("w", w, 0, MT)
+        load("x", x, 0, HALF)
         nc.sync.dma_start(
             out=b_rows[0:P:32, :].rearrange("q (a i) -> q a i", i=32),
             in_=b.rearrange("g (t q i) o -> q (g t) (i o)", t=TILES, i=32),
         )
-        nc.sync.dma_start(out=w_raw[:], in_=w.rearrange("g (p j) m -> (g p) j m", j=PACK))
-        nc.sync.dma_start(out=u_raw[:], in_=u.rearrange("g (p j) m -> (g p) j m", j=PACK))
+        load("x", x, 1, HALF)
+        load("u", u, 0, MT)
+        load("w", w, 1, MT)
+        load("u", u, 1, MT)
         res = {}
-        for g, t in order:
-            res[g, t] = sb.tile([P, N], F32, name="res_%d_%d" % (g, t))
-            nc.sync.dma_start(out=res[g, t][:], in_=r[g, t * MT:(t + 1) * MT, :])
+        for t in range(TILES):
+            res[t] = sb.tile([P, G, N], F32, name="res_%d" % t)
+            nc.sync.dma_start(out=res[t][:], in_=r[:, t * MT:(t + 1) * MT, :].rearrange("g p n -> p g n"))
 
-        x_lo = sb.tile([P, HALF, PACK], BF16, name="x_lo", align_bytes=64)
-        x_hi = sb.tile([P, HALF, PACK], BF16, name="x_hi", align_bytes=64)
         x_codes = sb.tile([P, N], U32, name="x_codes", align_bytes=64)
         x_scales = sb.tile([P, N], U8, name="x_scales", align_bytes=64)
-        interleave_vector(nc, x_raw[:, :, 0:HALF], x_lo[:])
-        interleave_scalar(nc, x_raw[:, :, HALF + X_VECTOR:N], x_hi[:, X_VECTOR:HALF, :])
-        interleave_vector(nc, x_raw[:, :, HALF:HALF + X_VECTOR], x_hi[:, 0:X_VECTOR, :])
-        nc.scalar.activation(out=b_half[:], in_=b_rows[:], func=ACT.Copy, scale=0.5)
-        quantize(nc, x_lo[:], x_codes[:, 0:HALF], x_scales[:, 0:HALF])
-        quantize(nc, x_hi[:], x_codes[:, HALF:N], x_scales[:, HALF:N])
-
-        grouped, codes, scales = {}, {}, {}
+        codes, scales = {}, {}
         for name in ("w", "u"):
             for t in range(TILES):
-                grouped[name, t] = sb.tile([P, MT, PACK], BF16, name="%s_bf_%d" % (name, t), align_bytes=64)
                 codes[name, t] = sb.tile([P, MT], U32, name="%s_codes_%d" % (name, t), align_bytes=64)
                 scales[name, t] = sb.tile([P, MT], U8, name="%s_scales_%d" % (name, t), align_bytes=64)
 
-        interleave_scalar(nc, w_raw[:, :, 0:MT], grouped["w", 0][:])
-        interleave_vector(nc, w_raw[:, :, MT:M], grouped["w", 1][:])
-        for t in range(TILES):
-            quantize(nc, grouped["w", t][:], codes["w", t][:], scales["w", t][:])
-        interleave_vector(nc, u_raw[:, :, 0:MT], grouped["u", 0][:])
-        interleave_scalar(nc, u_raw[:, :, MT:M], grouped["u", 1][:])
-        nc.vector.transpose(out=bias[:], in_=b_half[:])
-        for t in range(TILES):
-            quantize(nc, grouped["u", t][:], codes["u", t][:], scales["u", t][:])
+        def round_x(part, engine, lo, hi):
+            engine(nc, raw["x", part][:, :, lo:hi], grouped["x", part][:, lo:hi, :])
+
+        def quantize_x(part, lo, hi):
+            cols = slice(part * HALF + lo, part * HALF + hi)
+            quantize(nc, grouped["x", part][:, lo:hi, :], x_codes[:, cols], x_scales[:, cols])
+
+        def round_weights(name, t, engine):
+            engine(nc, raw[name, t][:], grouped[name, t][:])
+
+        def quantize_weights(name, t):
+            quantize(nc, grouped[name, t][:], codes[name, t][:], scales[name, t][:])
+
+        round_weights("w", 0, interleave_vector)
+        quantize_weights("w", 0)
+        for part in range(2):
+            round_x(part, interleave_vector, 0, QUARTER)
+            round_x(part, interleave_scalar, X_VECTOR, HALF)
+            round_x(part, interleave_vector, QUARTER, X_VECTOR)
+            quantize_x(part, 0, QUARTER)
+            quantize_x(part, QUARTER, HALF)
+            if part == 0:
+                nc.scalar.activation(out=b_half[:], in_=b_rows[:], func=ACT.Copy, scale=0.5)
+                nc.vector.transpose(out=bias[:], in_=b_half[:])
+        round_weights("u", 0, interleave_scalar)
+        quantize_weights("u", 0)
+        round_weights("w", 1, interleave_vector)
+        round_weights("u", 1, interleave_vector)
+        quantize_weights("w", 1)
+        quantize_weights("u", 1)
 
         acc = {}
 
@@ -117,15 +136,9 @@ def tile_rows_gglu_sigmoid_bias_res_kernel(tc, x, w, u, b, r, out):
                 stop=True,
             )
 
-        for name in ("w", "u"):
-            for g in range(G):
-                product(name, g, 0)
-        for g in range(G):
-            for name in ("w", "u"):
-                product(name, g, 1)
-
         gate, prod, y = {}, {}, {}
-        for g, t in order:
+
+        def activate(g, t):
             col = 32 * (g * TILES + t)
             gate[g, t] = sb.tile([P, N], F32, name="gate_%d_%d" % (g, t))
             nc.scalar.activation(
@@ -149,16 +162,27 @@ def tile_rows_gglu_sigmoid_bias_res_kernel(tc, x, w, u, b, r, out):
                 out=y[g, t][:, cols],
                 in0=prod[g, t][:, cols],
                 scalar=0.5,
-                in1=res[g, t][:, cols],
+                in1=res[t][:, g, cols],
                 op0=ALU.mult,
                 op1=ALU.add,
             )
             nc.sync.dma_start(out=out[g, t * MT:(t + 1) * MT, cols], in_=y[g, t][:, cols])
 
-        pieces = [(g, t, slice(0, N)) for g, t in order[:-1]]
-        pieces.extend([(*order[-1], slice(0, HALF)), (*order[-1], slice(HALF, N))])
-        multiply(*pieces[0])
-        for i in range(1, len(pieces)):
-            multiply(*pieces[i])
-            finish(*pieces[i - 1])
-        finish(*pieces[-1])
+        for t in range(TILES):
+            for name in ("w", "u"):
+                for g in range(G):
+                    product(name, g, t)
+            for g in range(G):
+                activate(g, t)
+
+        whole, left, right = slice(0, N), slice(0, HALF), slice(HALF, N)
+        for g in range(G):
+            multiply(g, 0, whole)
+        for g in range(G):
+            finish(g, 0, whole)
+        multiply(0, 1, whole)
+        multiply(1, 1, left)
+        finish(0, 1, whole)
+        multiply(1, 1, right)
+        finish(1, 1, left)
+        finish(1, 1, right)

from contextlib import ExitStack

import concourse.mybir as mybir

G, D, M, N = 2, 256, 256, 512
FLOPS = 2 * 2 * G * D * M * N

F32 = mybir.dt.float32
BF16 = mybir.dt.bfloat16
U32 = mybir.dt.uint32
U8 = mybir.dt.uint8
FP8X4 = mybir.dt.float8_e4m3fn_x4
ACT = mybir.ActivationFunctionType
ALU = mybir.AluOpType

P = 128
PACK = 4
ROWS = D // PACK
MT = 128
TILES = M // MT
HALF = N // 2
QUARTER = N // 4
X_VECTOR = 192


def walk(raw, grouped):
    src = raw.rearrange("p j (c i) -> p c j i", i=4)
    dst = grouped.rearrange("p (c i) j -> p c j i", i=4)
    return dst, src


def interleave_vector(nc, raw, grouped):
    dst, src = walk(raw, grouped)
    nc.vector.tensor_copy(out=dst, in_=src)


def interleave_scalar(nc, raw, grouped):
    dst, src = walk(raw, grouped)
    nc.scalar.copy(out=dst, in_=src)


def quantize(nc, grouped, codes, scales):
    nc.vector.quantize_mx(
        out=codes.bitcast(FP8X4),
        scales=scales,
        in_=grouped.rearrange("p c j -> p (c j)"),
    )


def tile_rows_gglu_sigmoid_bias_res_kernel(tc, x, w, u, b, r, out):
    nc = tc.nc
    with ExitStack() as ctx:
        sb = ctx.enter_context(tc.tile_pool(name="sb", bufs=1))
        ps = ctx.enter_context(tc.psum_pool(name="ps", bufs=1))
        ctx.enter_context(tc.manual_schedule())

        b_rows = sb.tile([P, P], F32, name="b_rows", align_bytes=64)
        b_half = sb.tile([P, P], F32, name="b_half", align_bytes=64)
        bias = sb.tile([P, P], F32, name="bias", align_bytes=64)
        nc.vector.memset(b_rows[:], 0.0)

        raw, grouped = {}, {}

        def load(name, src, part, width):
            raw[name, part] = sb.tile([P, PACK, width], F32, name="%s_raw_%d" % (name, part))
            grouped[name, part] = sb.tile([P, width, PACK], BF16, name="%s_bf_%d" % (name, part), align_bytes=64)
            rows = src.rearrange("g (p j) c -> (g p) j c", j=PACK)
            nc.sync.dma_start(out=raw[name, part][:], in_=rows[:, :, part * width:(part + 1) * width])

        load("w", w, 0, MT)
        load("x", x, 0, HALF)
        nc.sync.dma_start(
            out=b_rows[0:P:32, :].rearrange("q (a i) -> q a i", i=32),
            in_=b.rearrange("g (t q i) o -> q (g t) (i o)", t=TILES, i=32),
        )
        load("x", x, 1, HALF)
        load("u", u, 0, MT)
        load("w", w, 1, MT)
        load("u", u, 1, MT)
        res = {}
        for t in range(TILES):
            res[t] = sb.tile([P, G, N], F32, name="res_%d" % t)
            nc.sync.dma_start(out=res[t][:], in_=r[:, t * MT:(t + 1) * MT, :].rearrange("g p n -> p g n"))

        x_codes = sb.tile([P, N], U32, name="x_codes", align_bytes=64)
        x_scales = sb.tile([P, N], U8, name="x_scales", align_bytes=64)
        codes, scales = {}, {}
        for name in ("w", "u"):
            for t in range(TILES):
                codes[name, t] = sb.tile([P, MT], U32, name="%s_codes_%d" % (name, t), align_bytes=64)
                scales[name, t] = sb.tile([P, MT], U8, name="%s_scales_%d" % (name, t), align_bytes=64)

        def round_x(part, engine, lo, hi):
            engine(nc, raw["x", part][:, :, lo:hi], grouped["x", part][:, lo:hi, :])

        def quantize_x(part, lo, hi):
            cols = slice(part * HALF + lo, part * HALF + hi)
            quantize(nc, grouped["x", part][:, lo:hi, :], x_codes[:, cols], x_scales[:, cols])

        def round_weights(name, t, engine):
            engine(nc, raw[name, t][:], grouped[name, t][:])

        def quantize_weights(name, t):
            quantize(nc, grouped[name, t][:], codes[name, t][:], scales[name, t][:])

        round_weights("w", 0, interleave_vector)
        quantize_weights("w", 0)
        for part in range(2):
            round_x(part, interleave_vector, 0, QUARTER)
            round_x(part, interleave_scalar, X_VECTOR, HALF)
            round_x(part, interleave_vector, QUARTER, X_VECTOR)
            quantize_x(part, 0, QUARTER)
            quantize_x(part, QUARTER, HALF)
            if part == 0:
                nc.scalar.activation(out=b_half[:], in_=b_rows[:], func=ACT.Copy, scale=0.5)
                nc.vector.transpose(out=bias[:], in_=b_half[:])
        round_weights("u", 0, interleave_scalar)
        quantize_weights("u", 0)
        round_weights("w", 1, interleave_vector)
        round_weights("u", 1, interleave_vector)
        quantize_weights("w", 1)
        quantize_weights("u", 1)

        acc = {}

        def product(name, g, t):
            rows = slice(g * ROWS, (g + 1) * ROWS)
            acc[name, g, t] = ps.tile([P, N], F32, name="acc_%s_%d_%d" % (name, g, t))
            nc.tensor.matmul_mx(
                out=acc[name, g, t][:],
                lhsT=codes[name, t][rows, :].bitcast(FP8X4),
                lhsT_scale=scales[name, t][rows, :],
                rhs=x_codes[rows, :].bitcast(FP8X4),
                rhs_scale=x_scales[rows, :],
                start=True,
                stop=True,
            )

        gate, prod, y = {}, {}, {}

        def activate(g, t):
            col = 32 * (g * TILES + t)
            gate[g, t] = sb.tile([P, N], F32, name="gate_%d_%d" % (g, t))
            nc.scalar.activation(
                out=gate[g, t][:], in_=acc["w", g, t][:], func=ACT.Tanh, bias=bias[:, col:col + 1], scale=0.5
            )
            prod[g, t] = sb.tile([P, N], F32, name="prod_%d_%d" % (g, t))
            y[g, t] = sb.tile([P, N], F32, name="y_%d_%d" % (g, t))

        def multiply(g, t, cols):
            nc.vector.scalar_tensor_tensor(
                out=prod[g, t][:, cols],
                in0=gate[g, t][:, cols],
                scalar=1.0,
                in1=acc["u", g, t][:, cols],
                op0=ALU.add,
                op1=ALU.mult,
            )

        def finish(g, t, cols):
            nc.vector.scalar_tensor_tensor(
                out=y[g, t][:, cols],
                in0=prod[g, t][:, cols],
                scalar=0.5,
                in1=res[t][:, g, cols],
                op0=ALU.mult,
                op1=ALU.add,
            )
            nc.sync.dma_start(out=out[g, t * MT:(t + 1) * MT, cols], in_=y[g, t][:, cols])

        for t in range(TILES):
            for name in ("w", "u"):
                for g in range(G):
                    product(name, g, t)
            for g in range(G):
                activate(g, t)

        whole, left, right = slice(0, N), slice(0, HALF), slice(HALF, N)
        for g in range(G):
            multiply(g, 0, whole)
        for g in range(G):
            finish(g, 0, whole)
        multiply(0, 1, whole)
        multiply(1, 1, left)
        finish(0, 1, whole)
        multiply(1, 1, right)
        finish(1, 1, left)
        finish(1, 1, right)
